import numpy as np
import ml_dtypes


def mxq(x, axis, fmt="e4m3"):
    dtype, down = {"e4m3": (ml_dtypes.float8_e4m3fn, 7), "e5m2": (ml_dtypes.float8_e5m2, 14)}[fmt]
    v = np.moveaxis(np.asarray(x, np.float32).astype(ml_dtypes.bfloat16).astype(np.float64), axis, -1)
    blocks = v.reshape(v.shape[:-1] + (-1, 32))
    amax = np.abs(blocks).max(-1, keepdims=True)
    byte = np.maximum(np.where(amax > 0, np.frexp(amax)[1] - 1 + 127, 0) - down, 1)
    scale = np.exp2(byte - 127.0)
    codes = (blocks / scale).astype(np.float32).astype(dtype).astype(np.float64)
    return np.moveaxis((codes * scale).reshape(v.shape), -1, axis)


WIDE = False


def mx_kscale(k):
    if not WIDE:
        return np.ones(k)
    levels = np.array([10, -10, 5, -5, 0])
    if k % 512:
        return np.exp2(np.random.permutation(np.resize(levels, k // 32))).repeat(32)
    a = np.empty((k // 512, 16))
    for p in range(k // 512):
        a[p, :8] = np.random.permutation(np.resize(levels, 8))
        for g in range(8):
            far = levels[np.abs(levels - a[p, g]) >= 10]
            a[p, g + 8] = far[np.random.randint(len(far))]
    return np.exp2(a.ravel()).repeat(32)


def f64(x):
    return np.asarray(x).astype(np.float64)


def striped(idx):
    return np.tile(idx.reshape(-1, 16).T, (8, 1)).astype(np.uint16)


def unstriped(offs):
    return offs[:16].T.reshape(-1).astype(np.int64)


E2M1 = np.array([0.0, 0.5, 1.0, 1.5, 2.0, 3.0, 4.0, 6.0, -0.0, -0.5, -1.0, -1.5, -2.0, -3.0, -4.0, -6.0])


def pack_weight(w, fmt):
    k, n = w.shape
    w = f64(np.asarray(w, np.float32).astype(ml_dtypes.bfloat16)).reshape(k // 32, 32, n)
    amax = np.abs(w).max(1)
    if fmt == "e4m3":
        byte = np.frexp(amax)[1] - 1 + 127 - 7
    else:
        mant, ex = np.frexp(amax / 6.0)
        byte = np.where(mant > 0.5, ex, ex - 1) + 127
    byte = np.clip(np.where(amax > 0, byte, 1), 1, 254)
    scaled = (w * np.exp2(127.0 - byte)[:, None, :]).reshape(k, n).astype(np.float32)
    by_word = np.ascontiguousarray(scaled.reshape(k // 512, 128, 4, n).transpose(0, 1, 3, 2))
    if fmt == "e4m3":
        words = by_word.astype(ml_dtypes.float8_e4m3fn).view(np.uint8)
    else:
        c = by_word.astype(ml_dtypes.float4_e2m1fn).view(np.uint8) & 0xF
        words = (c[..., 0::2] | (c[..., 1::2] << 4)).reshape(k // 512, 128, 2 * n)
    return np.ascontiguousarray(words), np.ascontiguousarray(byte.astype(np.uint8).reshape(k // 512, 16, n))


def unpack_weight(words, scales, fmt):
    g, _, n = scales.shape
    words = np.ascontiguousarray(words).reshape(g, 128, n, -1)
    if fmt == "e4m3":
        vals = words.view(ml_dtypes.float8_e4m3fn).astype(np.float64)
    else:
        nib = np.empty((g, 128, n, 4), np.uint8)
        nib[..., 0::2] = words & 0xF
        nib[..., 1::2] = words >> 4
        vals = E2M1[nib]
    vals = vals * np.repeat(np.exp2(scales.astype(np.float64) - 127.0), 8, axis=1)[..., None]
    return vals.transpose(0, 1, 3, 2).reshape(g * 512, n)


def gelu(v):
    return 0.5 * v * (1.0 + np.tanh(np.sqrt(2.0 / np.pi) * (v + 0.044715 * v**3)))


def often(T, S):
    return np.random.permutation(T)[(T * np.random.uniform(0, 1, S) ** 4).astype(np.int64)]


T, S, K, K2, H, N = 4096, 1024, 1024, 512, 1024, 512

def setup_inputs():
    n = np.random.standard_normal
    s = mx_kscale(K)[:, None]
    s2 = mx_kscale(K2)[:, None]
    u = mx_kscale(H)[:, None]
    tab_words, tab_scales = pack_weight(n((K, T)) * s, "e4m3")
    tab2_words, tab2_scales = pack_weight(n((K2, T)) * s2, "e2m1")
    w4_words, w4_scales = pack_weight(n((K, H)) / np.sqrt(K) / s, "e2m1")
    x8_words, x8_scales = pack_weight(n((H, N)) / np.sqrt(H) / u, "e4m3")
    return {
        "tab_words": tab_words, "tab_scales": tab_scales,
        "tab2_words": tab2_words, "tab2_scales": tab2_scales,
        "offs": striped(often(T, S)),
        "offs2": striped(often(T, S)),
        "w4_words": w4_words, "w4_scales": w4_scales,
        "wr": (n((K2, H)) / np.sqrt(K2) / s2).astype(np.float32),
        "x8_words": x8_words, "x8_scales": x8_scales,
        "floor": np.random.uniform(0.2, 0.6, H).astype(np.float32),
        "gain": (np.exp(0.3 * n(H)) * u[:, 0]).astype(np.float32),
        "det": np.random.uniform(0.1, 0.4, N).astype(np.float32),
    }

def reference(tab_words, tab_scales, tab2_words, tab2_scales, offs, offs2, w4_words, w4_scales, wr, x8_words, x8_scales, floor, gain, det):
    v = unpack_weight(tab_words, tab_scales, "e4m3")[:, unstriped(offs)]
    v2 = unpack_weight(tab2_words, tab2_scales, "e2m1")[:, unstriped(offs2)]
    a = unpack_weight(w4_words, w4_scales, "e2m1").T @ v
    b = mxq(f64(wr), 0, "e4m3").T @ v2
    ab = np.concatenate([a, b], axis=1)
    lp = np.log(np.square(ab) + f64(floor)[:, None])
    h = f64(gain)[:, None] * (lp[:, :S] - lp[:, S:])
    y = unpack_weight(x8_words, x8_scales, "e4m3").T @ mxq(h, 0, "e4m3")
    return np.maximum(y, f64(det)[:, None])

@@ -1,0 +1,274 @@
+from contextlib import ExitStack
+
+import concourse.mybir as mybir
+
+T, S, K, K2, H, N = 4096, 1024, 1024, 512, 1024, 512
+FLOPS = 2 * S * (K * H + K2 * H + H * N)
+
+F32 = mybir.dt.float32
+BF16 = mybir.dt.bfloat16
+I32 = mybir.dt.int32
+U32 = mybir.dt.uint32
+U16 = mybir.dt.uint16
+U8 = mybir.dt.uint8
+FP8X4 = mybir.dt.float8_e4m3fn_x4
+FP4X4 = mybir.dt.float4_e2m1fn_x4
+ALU = mybir.AluOpType
+ACT = mybir.ActivationFunctionType
+
+P = 128
+PACK = 4
+PASS = P * PACK
+HALF = 512
+QUARTER = 256
+
+
+def tile_list_plume_retrieval_kernel(
+    tc, tab_words, tab_scales, tab2_words, tab2_scales, offs, offs2,
+    w4_words, w4_scales, wr, x8_words, x8_scales, floor, gain, det, out,
+):
+    nc = tc.nc
+    with ExitStack() as ctx:
+        keep = ctx.enter_context(tc.tile_pool(name="keep", bufs=1))
+        ring = ctx.enter_context(tc.tile_pool(name="ring", bufs=4))
+        stage = ctx.enter_context(tc.tile_pool(name="stage", bufs=1))
+        early = ctx.enter_context(tc.tile_pool(name="early", bufs=1))
+        psum = ctx.enter_context(tc.psum_pool(name="psum", bufs=1))
+
+        def held(shape, dtype, name, tag=None):
+            return keep.tile(shape, dtype, name=name, tag=tag or name, align_bytes=64)
+
+        banks = [psum.tile([P, HALF], F32, name="bank%d" % i) for i in range(8)]
+
+        list2 = keep.tile([P, S // 16], U16, name="list2")
+        list1 = keep.tile([P, S // 16], U16, name="list1")
+        tab2_s = held([P, T], U8, "tab2_s")
+        tab2_w = held([P, T], U16, "tab2_w")
+        tab_s = held([P, T], U8, "tab_s")
+        tab_w0 = held([P, T], U32, "tab_w0")
+        tab_w1 = stage.tile([P, T], U32, name="tab_w1", offset=12288, align_bytes=64)
+        tab_w = [tab_w0, tab_w1]
+        w4_s_raw = held([P, 2, H], U8, "w4_s_raw")
+        x8_s = held([P, 2, N], U8, "x8_s")
+        v_s = held([P, 2, S], U8, "v_s")
+        floor_sb = held([P, 2, PACK], F32, "floor_sb")
+        gain_sb = held([P, 2, PACK], F32, "gain_sb")
+        neg_det = held([P, 4], F32, "neg_det")
+
+        one = held([P, 1], F32, "one")
+        warm = held([P, 1], F32, "warm")
+        nc.vector.memset(tab2_s[:].bitcast(I32), 0)
+        nc.vector.memset(one[:], 1.0)
+        nc.vector.memset(tab_s[:].bitcast(I32), 0)
+
+        def load_wr(g):
+            raw = stage.tile([P, PACK, PASS], F32, name="wr_raw%d" % g, offset=6144 * (1 - g), align_bytes=64)
+            nc.sync.dma_start(out=raw[:], in_=wr[:, g * PASS:(g + 1) * PASS].rearrange("(p j) c -> p j c", j=PACK))
+            return raw
+
+        def load_tab(a):
+            nc.sync.dma_start(
+                out=tab_w[a][:].bitcast(I32), in_=tab_words[a].rearrange("p t i -> p (t i)").bitcast(I32))
+
+        nc.sync.dma_start(list2[:], offs2)
+        nc.gpsimd.dma_start(out=floor_sb[:], in_=floor.rearrange("(g p t) -> p g t", g=2, t=PACK))
+        nc.gpsimd.dma_start(out=gain_sb[:], in_=gain.rearrange("(g p t) -> p g t", g=2, t=PACK))
+        wr_raw0 = load_wr(0)
+        for r in range(4):
+            nc.scalar.dma_start(out=tab2_s[r:P:32, :].bitcast(I32), in_=tab2_scales[0, r:16:4, :].bitcast(I32))
+        nc.scalar.activation(warm[:], one[:], ACT.Ln)
+        nc.sync.dma_start(out=tab2_w[:].bitcast(I32), in_=tab2_words[0].bitcast(I32))
+        nc.sync.dma_start(list1[:], offs)
+        load_tab(0)
+        nc.scalar.dma_start(
+            out=tab_s[0:P:4, :].bitcast(I32), in_=tab_scales.rearrange("a q t -> (a q) t").bitcast(I32))
+        for plane in (v_s, w4_s_raw, x8_s):
+            nc.gpsimd.memset(plane[:].rearrange("p a c -> p (a c)").bitcast(I32), 0)
+        for raw_plane, scales in ((w4_s_raw, w4_scales), (x8_s, x8_scales)):
+            for r in range(4):
+                nc.gpsimd.dma_start(
+                    out=raw_plane[r:P:32, :, :].bitcast(I32),
+                    in_=scales[:, r:16:4, :].rearrange("a q c -> q a c").bitcast(I32))
+
+        def gather(window, offsets, dtype, name, place=None):
+            shape = [P, 16 * offsets.shape[1]]
+            if place is None:
+                picked = held(shape, dtype, name)
+            else:
+                picked = early.tile(shape, dtype, name=name, offset=place, align_bytes=64)
+            nc.vector.tensor_copy(picked[:], window.indirect(offsets))
+            return picked
+
+        def half_of(offsets, jh):
+            return offsets[:, jh * (HALF // 16):(jh + 1) * (HALF // 16)]
+
+        def wr_views(raw, grouped, first, count):
+            dst = grouped[:].rearrange("p (t m j) -> p m j t", t=count, j=PACK)
+            src = raw[:].rearrange("p j (m t) -> p m j t", t=PACK)[:, :, :, first:first + count]
+            return dst, src
+
+        def quantise(values, name):
+            width = values.shape[1] // PACK
+            codes = held([P, width], U32, name + "_codes")
+            scales = held([P, width], U8, name + "_scales")
+            nc.vector.quantize_mx(out=codes[:].bitcast(FP8X4), scales=scales[:], in_=values)
+            return codes, scales
+
+        v2_s = [None, None]
+        v2_w = [None, None]
+        v2_s[0] = gather(tab2_s[:], half_of(list2, 0), U8, "v2_s0")
+        pairs = [early.tile([P, 2 * PASS], BF16, name="wr_pair%d" % u, offset=2048 * u, align_bytes=64) for u in range(2)]
+        for u in range(2):
+            nc.scalar.activation(*wr_views(wr_raw0, pairs[u], 2 * u, 2), ACT.Copy)
+        wr_raw1 = load_wr(1)
+        w4_raw = stage.tile([P, 2, H], U16, name="w4_raw", offset=8192, align_bytes=64)
+        nc.sync.dma_start(out=w4_raw[:].bitcast(I32), in_=w4_words.rearrange("a p c -> p a c").bitcast(I32))
+        load_tab(1)
+        wr_q = [[quantise(pairs[0][:], "wr00")]]
+        v2_w[0] = gather(tab2_w[:], half_of(list2, 0), U16, "v2_w0")
+        wr_q[0].append(quantise(pairs[1][:], "wr01"))
+        v2_s[1] = gather(tab2_s[:], half_of(list2, 1), U8, "v2_s1", 3072)
+        v2_w[1] = gather(tab2_w[:], half_of(list2, 1), U16, "v2_w1", 2048)
+        wr_grouped = held([P, PASS * PACK], BF16, "wr_grouped")
+        nc.vector.tensor_copy(*wr_views(wr_raw1, wr_grouped, 0, PACK))
+        wr_q.append([quantise(wr_grouped[:], "wr1")])
+
+        picked_s = gather(tab_s[:], list1[:], U8, "picked_s", 3584)
+        for a in range(2):
+            for r in range(4):
+                nc.sync.dma_start(
+                    out=v_s[r:P:32, a, :].bitcast(I32),
+                    in_=picked_s[64 * a + 4 * r:64 * a + 64:16, :].bitcast(I32))
+        w4_s = held([P, 2 * H], U8, "w4_s", tag="wr_grouped")
+        nc.vector.tensor_copy(
+            w4_s[:].rearrange("p (u t m) -> p u t m", t=PACK, m=P),
+            w4_s_raw[:].rearrange("p a (g m t) -> p (a g) t m", t=PACK, m=P))
+        v_w = [[gather(tab_w[a][:], half_of(list1, 0), U32, "v_w0%d" % a) for a in range(2)]]
+        w4_w = held([P, 2 * H], U16, "w4_w")
+        nc.vector.tensor_copy(
+            w4_w[:].rearrange("p (u t m) -> p u t m", t=PACK, m=P),
+            w4_raw[:].rearrange("p a (g m t) -> p (a g) t m", t=PACK, m=P))
+        v_w.append([gather(tab_w[a][:], half_of(list1, 1), U32, "v_w1%d" % a) for a in range(2)])
+        x8_w = stage.tile([P, 2, N], U32, name="x8_w", offset=0, align_bytes=64)
+        nc.sync.dma_start(out=x8_w[:].bitcast(I32), in_=x8_words.rearrange("a p c i -> p a (c i)").bitcast(I32))
+        det_sb = early.tile([P, 4], F32, name="det_sb", offset=4096, align_bytes=64)
+        with nc.allow_non_contiguous_dma(reason="one detection limit a partition"):
+            nc.sync.dma_start(out=det_sb[:], in_=det.rearrange("(c p) -> p c", p=P))
+        nc.gpsimd.tensor_scalar(neg_det[:], det_sb[:], -1.0, 0.0, ALU.mult, ALU.add)
+
+        turn = [0]
+
+        def next_bank():
+            turn[0] = (turn[0] + 1) % 4
+            return banks[turn[0]]
+
+        def product_b(g, t, jh):
+            bank = next_bank()
+            per_tile = PACK // len(wr_q[g])
+            codes, scales = wr_q[g][t // per_tile]
+            cols = slice(t % per_tile * P, (t % per_tile + 1) * P)
+            nc.tensor.matmul_mx(
+                out=bank[:], lhsT=codes[:, cols].bitcast(FP8X4), lhsT_scale=scales[:, cols],
+                rhs=v2_w[jh][:].bitcast(FP4X4), rhs_scale=v2_s[jh][:], start=True, stop=True)
+            return bank
+
+        def product_a(g, t, jh):
+            bank = next_bank()
+            for a in range(2):
+                first = a * H + g * PASS + t * P
+                cols = slice(first, first + P)
+                nc.tensor.matmul_mx(
+                    out=bank[:], lhsT=w4_w[:, cols].bitcast(FP4X4), lhsT_scale=w4_s[:, cols],
+                    rhs=v_w[jh][a][:].bitcast(FP8X4), rhs_scale=v_s[:, a, jh * HALF:(jh + 1) * HALF],
+                    start=(a == 0), stop=(a == 1))
+            return bank
+
+        def square(product, g, t, jh):
+            power = ring.tile([P, HALF], F32, name="power", bufs=6)
+            nc.scalar.activation(power[:], product(g, t, jh)[:], ACT.Square)
+            return power
+
+        ref_log = [[held([P, S], F32, "ref_log%d%d" % (g, t)) for t in range(PACK)] for g in range(2)]
+
+        def finish_b(g, t, jh, power):
+            dst = ref_log[g][t][:, jh * HALF:(jh + 1) * HALF]
+            nc.scalar.activation(dst, power[:], ACT.Ln, bias=floor_sb[:, g, t:t + 1])
+            nc.vector.tensor_scalar(dst, dst, gain_sb[:, g, t:t + 1], None, ALU.mult)
+
+        def finish_a(g, t, first, power, planes):
+            width = power.shape[1]
+            log_a = ring.tile([P, width], F32, name="log_a", bufs=8)
+            nc.scalar.activation(log_a[:], power, ACT.Ln, bias=floor_sb[:, g, t:t + 1])
+            nc.vector.scalar_tensor_tensor(
+                planes[:, t, :], log_a[:], gain_sb[:, g, t:t + 1], ref_log[g][t][:, first:first + width],
+                ALU.mult, ALU.subtract)
+
+        def weave(planes, name):
+            width = planes.shape[2]
+            woven = keep.tile([P, width * PACK], BF16, name=name, tag="woven", bufs=2, align_bytes=64)
+            nc.vector.tensor_copy(
+                woven[:].rearrange("p (c i t) -> p c t i", i=4, t=PACK),
+                planes.rearrange("p t (c i) -> p c t i", i=4))
+            return quantise(woven[:], name)
+
+        def signals(c, g, h_q, h_cols, bank):
+            codes, scales = h_q
+            cols = slice(c * P, (c + 1) * P)
+            width = h_cols.stop - h_cols.start
+            nc.tensor.matmul_mx(
+                out=bank[:, 0:width], lhsT=x8_w[:, g, cols].bitcast(FP8X4), lhsT_scale=x8_s[:, g, cols],
+                rhs=codes[:, h_cols].bitcast(FP8X4), rhs_scale=scales[:, h_cols], start=(g == 0), stop=(g == 1))
+
+        def report(c, bank, first, width, on_scalar):
+            result = keep.tile([P, width], F32, name="result", tag="result", bufs=8)
+            if on_scalar:
+                excess = ring.tile([P, width], F32, name="excess")
+                nc.scalar.activation(excess[:], bank[:, 0:width], ACT.Relu, bias=neg_det[:, c:c + 1])
+                nc.scalar.activation(result[:], excess[:], ACT.Identity, bias=det_sb[:, c:c + 1])
+            else:
+                nc.vector.tensor_scalar(result[:], bank[:, 0:width], det_sb[:, c:c + 1], None, ALU.max)
+            nc.sync.dma_start(out=out[c * P:(c + 1) * P, first:first + width], in_=result[:])
+
+        h_q = {}
+
+        def finish(side, g, t, jh, power, planes):
+            if side == "b":
+                finish_b(g, t, jh, power)
+                return
+            finish_a(g, t, jh * HALF, power[:], planes)
+            if t == PACK - 1:
+                h_q[g, jh] = weave(planes[:], "h%d%d" % (g, jh))
+                if (g, jh) == (1, 0):
+                    for c in range(4):
+                        for g_pass in range(2):
+                            signals(c, g_pass, h_q[g_pass, 0], slice(0, HALF), banks[4 + c])
+            if (g, jh) == (0, 1):
+                report(t, banks[4 + t], 0, HALF, False)
+
+        order = [("b", 0, 0), ("b", 0, 1), ("b", 1, 0), ("a", 0, 0), ("a", 1, 0), ("a", 0, 1), ("b", 1, 1)]
+        waiting = None
+        for side, g, jh in order:
+            planes = ring.tile([P, PACK, HALF], BF16, name="planes", bufs=2) if side == "a" else None
+            for t in range(PACK):
+                power = square(product_a if side == "a" else product_b, g, t, jh)
+                if waiting is not None:
+                    finish(*waiting)
+                waiting = (side, g, t, jh, power, planes)
+        last = []
+        for t in range(PACK):
+            last.append(square(product_a, 1, t, 1))
+            if t == 0:
+                finish(*waiting)
+        for q in range(2):
+            planes = held([P, PACK, QUARTER], BF16, "planes_q%d" % q)
+            cols = slice(q * QUARTER, (q + 1) * QUARTER)
+            for t in range(PACK):
+                finish_a(1, t, HALF + q * QUARTER, last[t][:, cols], planes)
+            h1q = weave(planes[:], "h1q%d" % q)
+            for c in range(4):
+                signals(c, 0, h_q[0, 1], cols, banks[4 * q + c])
+            for c in range(4):
+                signals(c, 1, h1q, slice(0, QUARTER), banks[4 * q + c])
+        for q in range(2):
+            for c in range(4):
+                report(c, banks[4 * q + c], HALF + q * QUARTER, QUARTER, q == 0)

@@ -21,6 +21,8 @@ PACK = 4
 PASS = P * PACK
 HALF = 512
 QUARTER = 256
+ROW = S + H + N
+LIVE = 96
 
 
 def tile_list_plume_retrieval_kernel(
@@ -42,53 +44,44 @@ def tile_list_plume_retrieval_kernel(
 
         list2 = keep.tile([P, S // 16], U16, name="list2")
         list1 = keep.tile([P, S // 16], U16, name="list1")
-        tab2_s = held([P, T], U8, "tab2_s")
+        tab2_s = early.tile([P, T], U8, name="tab2_s", offset=4096, align_bytes=64)
         tab2_w = held([P, T], U16, "tab2_w")
         tab_s = held([P, T], U8, "tab_s")
-        tab_w0 = held([P, T], U32, "tab_w0")
-        tab_w1 = stage.tile([P, T], U32, name="tab_w1", offset=12288, align_bytes=64)
-        tab_w = [tab_w0, tab_w1]
-        w4_s_raw = held([P, 2, H], U8, "w4_s_raw")
-        x8_s = held([P, 2, N], U8, "x8_s")
-        v_s = held([P, 2, S], U8, "v_s")
-        floor_sb = held([P, 2, PACK], F32, "floor_sb")
-        gain_sb = held([P, 2, PACK], F32, "gain_sb")
+        weight_s = held([P, H + N], U8, "weight_s")
+        planes_s = held([P, 2, ROW], U8, "planes_s")
+        by_row = held([P, 2, 2, PACK], F32, "by_row")
+        floor_sb, gain_sb = by_row[:, 0], by_row[:, 1]
         neg_det = held([P, 4], F32, "neg_det")
 
-        one = held([P, 1], F32, "one")
-        warm = held([P, 1], F32, "warm")
+        warm = held([P, 4 * PACK], F32, "warm")
+        flat = by_row[:].rearrange("p u g t -> p (u g t)")
+        nc.vector.memset(flat, 1.0)
         nc.vector.memset(tab2_s[:].bitcast(I32), 0)
-        nc.vector.memset(one[:], 1.0)
-        nc.vector.memset(tab_s[:].bitcast(I32), 0)
+        nc.vector.memset(tab_s[0:LIVE, :].bitcast(I32), 0)
+        nc.vector.memset(weight_s[0:LIVE, :].bitcast(I32), 0)
 
         def load_wr(g):
             raw = stage.tile([P, PACK, PASS], F32, name="wr_raw%d" % g, offset=6144 * (1 - g), align_bytes=64)
             nc.sync.dma_start(out=raw[:], in_=wr[:, g * PASS:(g + 1) * PASS].rearrange("(p j) c -> p j c", j=PACK))
             return raw
 
-        def load_tab(a):
+        def load_tab(a, window):
             nc.sync.dma_start(
-                out=tab_w[a][:].bitcast(I32), in_=tab_words[a].rearrange("p t i -> p (t i)").bitcast(I32))
+                out=window[:].bitcast(I32), in_=tab_words[a].rearrange("p t i -> p (t i)").bitcast(I32))
+            return window
 
+        nc.sync.dma_start(list1[:], offs)
         nc.sync.dma_start(list2[:], offs2)
-        nc.gpsimd.dma_start(out=floor_sb[:], in_=floor.rearrange("(g p t) -> p g t", g=2, t=PACK))
-        nc.gpsimd.dma_start(out=gain_sb[:], in_=gain.rearrange("(g p t) -> p g t", g=2, t=PACK))
+        for rows, scales in ((tab_s[LIVE:P, :], tab_scales), (weight_s[LIVE:P, 0:H], w4_scales),
+                             (weight_s[LIVE:P, H:H + N], x8_scales)):
+            nc.scalar.dma_start(out=rows.bitcast(I32), in_=scales.rearrange("a q c -> (a q) c").bitcast(I32))
         wr_raw0 = load_wr(0)
+        nc.sync.dma_start(out=tab2_w[:].bitcast(I32), in_=tab2_words[0].bitcast(I32))
+        nc.scalar.activation(warm[:], flat, ACT.Ln)
         for r in range(4):
             nc.scalar.dma_start(out=tab2_s[r:P:32, :].bitcast(I32), in_=tab2_scales[0, r:16:4, :].bitcast(I32))
-        nc.scalar.activation(warm[:], one[:], ACT.Ln)
-        nc.sync.dma_start(out=tab2_w[:].bitcast(I32), in_=tab2_words[0].bitcast(I32))
-        nc.sync.dma_start(list1[:], offs)
-        load_tab(0)
-        nc.scalar.dma_start(
-            out=tab_s[0:P:4, :].bitcast(I32), in_=tab_scales.rearrange("a q t -> (a q) t").bitcast(I32))
-        for plane in (v_s, w4_s_raw, x8_s):
-            nc.gpsimd.memset(plane[:].rearrange("p a c -> p (a c)").bitcast(I32), 0)
-        for raw_plane, scales in ((w4_s_raw, w4_scales), (x8_s, x8_scales)):
-            for r in range(4):
-                nc.gpsimd.dma_start(
-                    out=raw_plane[r:P:32, :, :].bitcast(I32),
-                    in_=scales[:, r:16:4, :].rearrange("a q c -> q a c").bitcast(I32))
+        nc.scalar.dma_start(out=floor_sb, in_=floor.rearrange("(g p t) -> p g t", g=2, t=PACK))
+        nc.scalar.dma_start(out=gain_sb, in_=gain.rearrange("(g p t) -> p g t", g=2, t=PACK))
 
         def gather(window, offsets, dtype, name, place=None):
             shape = [P, 16 * offsets.shape[1]]
@@ -102,9 +95,9 @@ def tile_list_plume_retrieval_kernel(
         def half_of(offsets, jh):
             return offsets[:, jh * (HALF // 16):(jh + 1) * (HALF // 16)]
 
-        def wr_views(raw, grouped, first, count):
-            dst = grouped[:].rearrange("p (t m j) -> p m j t", t=count, j=PACK)
-            src = raw[:].rearrange("p j (m t) -> p m j t", t=PACK)[:, :, :, first:first + count]
+        def wr_views(raw, pair, u):
+            dst = pair.rearrange("p (t m j) -> p m j t", t=2, j=PACK)
+            src = raw[:].rearrange("p j (m t) -> p m j t", t=PACK)[:, :, :, 2 * u:2 * u + 2]
             return dst, src
 
         def quantise(values, name):
@@ -116,42 +109,47 @@ def tile_list_plume_retrieval_kernel(
 
         v2_s = [None, None]
         v2_w = [None, None]
+        picked_s = gather(tab_s[:], list1[:], U8, "picked_s")
+        tab_w = [load_tab(0, held([P, T], U32, "tab_w0", tag="tab_s"))]
         v2_s[0] = gather(tab2_s[:], half_of(list2, 0), U8, "v2_s0")
         pairs = [early.tile([P, 2 * PASS], BF16, name="wr_pair%d" % u, offset=2048 * u, align_bytes=64) for u in range(2)]
         for u in range(2):
-            nc.scalar.activation(*wr_views(wr_raw0, pairs[u], 2 * u, 2), ACT.Copy)
+            nc.scalar.activation(*wr_views(wr_raw0, pairs[u][:], u), ACT.Copy)
+        wr_q = [[quantise(pairs[0][:], "wr00")]]
         wr_raw1 = load_wr(1)
         w4_raw = stage.tile([P, 2, H], U16, name="w4_raw", offset=8192, align_bytes=64)
         nc.sync.dma_start(out=w4_raw[:].bitcast(I32), in_=w4_words.rearrange("a p c -> p a c").bitcast(I32))
-        load_tab(1)
-        wr_q = [[quantise(pairs[0][:], "wr00")]]
+        tab_w.append(load_tab(1, stage.tile([P, T], U32, name="tab_w1", offset=12288, align_bytes=64)))
         v2_w[0] = gather(tab2_w[:], half_of(list2, 0), U16, "v2_w0")
         wr_q[0].append(quantise(pairs[1][:], "wr01"))
-        v2_s[1] = gather(tab2_s[:], half_of(list2, 1), U8, "v2_s1", 3072)
-        v2_w[1] = gather(tab2_w[:], half_of(list2, 1), U16, "v2_w1", 2048)
-        wr_grouped = held([P, PASS * PACK], BF16, "wr_grouped")
-        nc.vector.tensor_copy(*wr_views(wr_raw1, wr_grouped, 0, PACK))
-        wr_q.append([quantise(wr_grouped[:], "wr1")])
-
-        picked_s = gather(tab_s[:], list1[:], U8, "picked_s", 3584)
+        v2_s[1] = gather(tab2_s[:], half_of(list2, 1), U8, "v2_s1", 2048)
+        v2_w[1] = gather(tab2_w[:], half_of(list2, 1), U16, "v2_w1", 4096)
+        rows_s = early.tile([P, ROW], U8, name="rows_s", offset=5120, align_bytes=64)
+        nc.vector.memset(planes_s[:].rearrange("p a c -> p (a c)").bitcast(I32), 0)
+        nc.vector.tensor_copy(
+            rows_s[:, S:S + H].rearrange("p (g t o i) -> p g o t i", g=2, t=PACK, i=16),
+            weight_s[:, 0:H].rearrange("p (g o i t) -> p g o t i", g=2, t=PACK, i=16))
+        nc.vector.tensor_copy(rows_s[:, 0:S].bitcast(I32), picked_s[:].bitcast(I32))
+        nc.vector.tensor_copy(rows_s[:, S + H:ROW].bitcast(I32), weight_s[:, H:H + N].bitcast(I32))
         for a in range(2):
             for r in range(4):
                 nc.sync.dma_start(
-                    out=v_s[r:P:32, a, :].bitcast(I32),
-                    in_=picked_s[64 * a + 4 * r:64 * a + 64:16, :].bitcast(I32))
-        w4_s = held([P, 2 * H], U8, "w4_s", tag="wr_grouped")
-        nc.vector.tensor_copy(
-            w4_s[:].rearrange("p (u t m) -> p u t m", t=PACK, m=P),
-            w4_s_raw[:].rearrange("p a (g m t) -> p (a g) t m", t=PACK, m=P))
+                    out=planes_s[r:P:32, a, :].bitcast(I32),
+                    in_=rows_s[LIVE + 16 * a + r:LIVE + 16 * (a + 1):4, :].bitcast(I32))
+        wr_grouped = held([P, PASS * PACK], BF16, "wr_grouped")
+        for u in range(2):
+            nc.vector.tensor_copy(*wr_views(wr_raw1, wr_grouped[:, 2 * PASS * u:2 * PASS * (u + 1)], u))
+        wr_q.append([quantise(wr_grouped[:], "wr1")])
+
         v_w = [[gather(tab_w[a][:], half_of(list1, 0), U32, "v_w0%d" % a) for a in range(2)]]
         w4_w = held([P, 2 * H], U16, "w4_w")
         nc.vector.tensor_copy(
-            w4_w[:].rearrange("p (u t m) -> p u t m", t=PACK, m=P),
-            w4_raw[:].rearrange("p a (g m t) -> p (a g) t m", t=PACK, m=P))
+            w4_w[:].rearrange("p (u t o i) -> p u o t i", u=4, t=PACK, i=8),
+            w4_raw[:].rearrange("p a (g o i t) -> p (a g) o t i", g=2, t=PACK, i=8))
         v_w.append([gather(tab_w[a][:], half_of(list1, 1), U32, "v_w1%d" % a) for a in range(2)])
         x8_w = stage.tile([P, 2, N], U32, name="x8_w", offset=0, align_bytes=64)
         nc.sync.dma_start(out=x8_w[:].bitcast(I32), in_=x8_words.rearrange("a p c i -> p a (c i)").bitcast(I32))
-        det_sb = early.tile([P, 4], F32, name="det_sb", offset=4096, align_bytes=64)
+        det_sb = early.tile([P, 4], F32, name="det_sb", offset=5120, align_bytes=64)
         with nc.allow_non_contiguous_dma(reason="one detection limit a partition"):
             nc.sync.dma_start(out=det_sb[:], in_=det.rearrange("(c p) -> p c", p=P))
         nc.gpsimd.tensor_scalar(neg_det[:], det_sb[:], -1.0, 0.0, ALU.mult, ALU.add)
@@ -175,17 +173,17 @@ def tile_list_plume_retrieval_kernel(
         def product_a(g, t, jh):
             bank = next_bank()
             for a in range(2):
-                first = a * H + g * PASS + t * P
-                cols = slice(first, first + P)
+                first = g * PASS + t * P
                 nc.tensor.matmul_mx(
-                    out=bank[:], lhsT=w4_w[:, cols].bitcast(FP4X4), lhsT_scale=w4_s[:, cols],
-                    rhs=v_w[jh][a][:].bitcast(FP8X4), rhs_scale=v_s[:, a, jh * HALF:(jh + 1) * HALF],
+                    out=bank[:], lhsT=w4_w[:, a * H + first:a * H + first + P].bitcast(FP4X4),
+                    lhsT_scale=planes_s[:, a, S + first:S + first + P],
+                    rhs=v_w[jh][a][:].bitcast(FP8X4), rhs_scale=planes_s[:, a, jh * HALF:(jh + 1) * HALF],
                     start=(a == 0), stop=(a == 1))
             return bank
 
-        def square(product, g, t, jh):
-            power = ring.tile([P, HALF], F32, name="power", bufs=6)
-            nc.scalar.activation(power[:], product(g, t, jh)[:], ACT.Square)
+        def square(amplitude):
+            power = ring.tile([P, amplitude.shape[1]], F32, name="power", bufs=6)
+            nc.scalar.activation(power[:], amplitude, ACT.Square)
             return power
 
         ref_log = [[held([P, S], F32, "ref_log%d%d" % (g, t)) for t in range(PACK)] for g in range(2)]
@@ -216,7 +214,7 @@ def tile_list_plume_retrieval_kernel(
             cols = slice(c * P, (c + 1) * P)
             width = h_cols.stop - h_cols.start
             nc.tensor.matmul_mx(
-                out=bank[:, 0:width], lhsT=x8_w[:, g, cols].bitcast(FP8X4), lhsT_scale=x8_s[:, g, cols],
+                out=bank[:, 0:width], lhsT=x8_w[:, g, cols].bitcast(FP8X4), lhsT_scale=planes_s[:, g, S + H + c * P:S + H + (c + 1) * P],
                 rhs=codes[:, h_cols].bitcast(FP8X4), rhs_scale=scales[:, h_cols], start=(g == 0), stop=(g == 1))
 
         def report(c, bank, first, width, on_scalar):
@@ -250,25 +248,26 @@ def tile_list_plume_retrieval_kernel(
         for side, g, jh in order:
             planes = ring.tile([P, PACK, HALF], BF16, name="planes", bufs=2) if side == "a" else None
             for t in range(PACK):
-                power = square(product_a if side == "a" else product_b, g, t, jh)
+                power = square((product_a if side == "a" else product_b)(g, t, jh)[:])
                 if waiting is not None:
                     finish(*waiting)
                 waiting = (side, g, t, jh, power, planes)
-        last = []
-        for t in range(PACK):
-            last.append(square(product_a, 1, t, 1))
-            if t == 0:
-                finish(*waiting)
+        last = [product_a(1, t, 1) for t in range(PACK)]
         for q in range(2):
             planes = held([P, PACK, QUARTER], BF16, "planes_q%d" % q)
             cols = slice(q * QUARTER, (q + 1) * QUARTER)
+            powers = []
             for t in range(PACK):
-                finish_a(1, t, HALF + q * QUARTER, last[t][:, cols], planes)
+                powers.append(square(last[t][:, cols]))
+                if (q, t) == (0, 0):
+                    finish(*waiting)
+            for t in range(PACK):
+                finish_a(1, t, HALF + q * QUARTER, powers[t][:], planes)
             h1q = weave(planes[:], "h1q%d" % q)
             for c in range(4):
-                signals(c, 0, h_q[0, 1], cols, banks[4 * q + c])
+                signals(c, 0, h_q[0, 1], cols, banks[4 * (1 - q) + c])
             for c in range(4):
-                signals(c, 1, h1q, slice(0, QUARTER), banks[4 * q + c])
+                signals(c, 1, h1q, slice(0, QUARTER), banks[4 * (1 - q) + c])
         for q in range(2):
             for c in range(4):
-                report(c, banks[4 * q + c], HALF + q * QUARTER, QUARTER, q == 0)
+                report(c, banks[4 * (1 - q) + c], HALF + q * QUARTER, QUARTER, q == 0)

@@ -45,7 +45,6 @@ def tile_list_plume_retrieval_kernel(
         list2 = keep.tile([P, S // 16], U16, name="list2")
         list1 = keep.tile([P, S // 16], U16, name="list1")
         tab2_s = early.tile([P, T], U8, name="tab2_s", offset=4096, align_bytes=64)
-        tab2_w = held([P, T], U16, "tab2_w")
         tab_s = held([P, T], U8, "tab_s")
         weight_s = held([P, H + N], U8, "weight_s")
         planes_s = held([P, 2, ROW], U8, "planes_s")
@@ -60,8 +59,7 @@ def tile_list_plume_retrieval_kernel(
         nc.vector.memset(tab_s[0:LIVE, :].bitcast(I32), 0)
         nc.vector.memset(weight_s[0:LIVE, :].bitcast(I32), 0)
 
-        def load_wr(g):
-            raw = stage.tile([P, PACK, PASS], F32, name="wr_raw%d" % g, offset=6144 * (1 - g), align_bytes=64)
+        def load_wr(g, raw):
             nc.sync.dma_start(out=raw[:], in_=wr[:, g * PASS:(g + 1) * PASS].rearrange("(p j) c -> p j c", j=PACK))
             return raw
 
@@ -75,7 +73,8 @@ def tile_list_plume_retrieval_kernel(
         for rows, scales in ((tab_s[LIVE:P, :], tab_scales), (weight_s[LIVE:P, 0:H], w4_scales),
                              (weight_s[LIVE:P, H:H + N], x8_scales)):
             nc.scalar.dma_start(out=rows.bitcast(I32), in_=scales.rearrange("a q c -> (a q) c").bitcast(I32))
-        wr_raw0 = load_wr(0)
+        wr_raw0 = load_wr(0, stage.tile([P, PACK, PASS], F32, name="wr_raw0", offset=14336, align_bytes=64))
+        tab2_w = held([P, T], U16, "tab2_w")
         nc.sync.dma_start(out=tab2_w[:].bitcast(I32), in_=tab2_words[0].bitcast(I32))
         nc.scalar.activation(warm[:], flat, ACT.Ln)
         for r in range(4):
@@ -110,16 +109,16 @@ def tile_list_plume_retrieval_kernel(
         v2_s = [None, None]
         v2_w = [None, None]
         picked_s = gather(tab_s[:], list1[:], U8, "picked_s")
-        tab_w = [load_tab(0, held([P, T], U32, "tab_w0", tag="tab_s"))]
+        wr_raw1 = load_wr(1, held([P, PACK, PASS], F32, "wr_raw1", tag="tab_s"))
         v2_s[0] = gather(tab2_s[:], half_of(list2, 0), U8, "v2_s0")
         pairs = [early.tile([P, 2 * PASS], BF16, name="wr_pair%d" % u, offset=2048 * u, align_bytes=64) for u in range(2)]
         for u in range(2):
             nc.scalar.activation(*wr_views(wr_raw0, pairs[u][:], u), ACT.Copy)
         wr_q = [[quantise(pairs[0][:], "wr00")]]
-        wr_raw1 = load_wr(1)
-        w4_raw = stage.tile([P, 2, H], U16, name="w4_raw", offset=8192, align_bytes=64)
+        tab_w = [load_tab(0, stage.tile([P, T], U32, name="tab_w0", offset=0, align_bytes=64))]
+        w4_raw = stage.tile([P, 2, H], U16, name="w4_raw", offset=16384, align_bytes=64)
         nc.sync.dma_start(out=w4_raw[:].bitcast(I32), in_=w4_words.rearrange("a p c -> p a c").bitcast(I32))
-        tab_w.append(load_tab(1, stage.tile([P, T], U32, name="tab_w1", offset=12288, align_bytes=64)))
+        tab_w.append(load_tab(1, stage.tile([P, T], U32, name="tab_w1", offset=20480, align_bytes=64)))
         v2_w[0] = gather(tab2_w[:], half_of(list2, 0), U16, "v2_w0")
         wr_q[0].append(quantise(pairs[1][:], "wr01"))
         v2_s[1] = gather(tab2_s[:], half_of(list2, 1), U8, "v2_s1", 2048)
@@ -133,7 +132,7 @@ def tile_list_plume_retrieval_kernel(
         nc.vector.tensor_copy(rows_s[:, S + H:ROW].bitcast(I32), weight_s[:, H:H + N].bitcast(I32))
         for a in range(2):
             for r in range(4):
-                nc.sync.dma_start(
+                (nc.sync if r < 3 else nc.gpsimd).dma_start(
                     out=planes_s[r:P:32, a, :].bitcast(I32),
                     in_=rows_s[LIVE + 16 * a + r:LIVE + 16 * (a + 1):4, :].bitcast(I32))
         wr_grouped = held([P, PASS * PACK], BF16, "wr_grouped")
@@ -147,7 +146,7 @@ def tile_list_plume_retrieval_kernel(
             w4_w[:].rearrange("p (u t o i) -> p u o t i", u=4, t=PACK, i=8),
             w4_raw[:].rearrange("p a (g o i t) -> p (a g) o t i", g=2, t=PACK, i=8))
         v_w.append([gather(tab_w[a][:], half_of(list1, 1), U32, "v_w1%d" % a) for a in range(2)])
-        x8_w = stage.tile([P, 2, N], U32, name="x8_w", offset=0, align_bytes=64)
+        x8_w = stage.tile([P, 2, N], U32, name="x8_w", offset=16384, align_bytes=64)
         nc.sync.dma_start(out=x8_w[:].bitcast(I32), in_=x8_words.rearrange("a p c i -> p a (c i)").bitcast(I32))
         det_sb = early.tile([P, 4], F32, name="det_sb", offset=5120, align_bytes=64)
         with nc.allow_non_contiguous_dma(reason="one detection limit a partition"):
@@ -188,22 +187,30 @@ def tile_list_plume_retrieval_kernel(
 
         ref_log = [[held([P, S], F32, "ref_log%d%d" % (g, t)) for t in range(PACK)] for g in range(2)]
 
+        weighted = [
+            [stage.tile([P, S], F32, name="weighted%d%d" % (g, t), offset=20480 * g + 4096 * t, align_bytes=64)
+             for t in range(PACK)] for g in range(2)]
+
         def finish_b(g, t, jh, power):
-            dst = ref_log[g][t][:, jh * HALF:(jh + 1) * HALF]
-            nc.scalar.activation(dst, power[:], ACT.Ln, bias=floor_sb[:, g, t:t + 1])
-            nc.vector.tensor_scalar(dst, dst, gain_sb[:, g, t:t + 1], None, ALU.mult)
+            log_b = ref_log[g][t]
+            cols = slice(jh * HALF, (jh + 1) * HALF)
+            nc.scalar.activation(log_b[:, cols], power[:], ACT.Ln, bias=floor_sb[:, g, t:t + 1])
+            if (g, jh) != (0, 0):
+                ready = slice(0, S) if g == 0 else cols
+                nc.vector.tensor_scalar(
+                    weighted[g][t][:, ready], log_b[:, ready], gain_sb[:, g, t:t + 1], None, ALU.mult)
 
         def finish_a(g, t, first, power, planes):
             width = power.shape[1]
             log_a = ring.tile([P, width], F32, name="log_a", bufs=8)
             nc.scalar.activation(log_a[:], power, ACT.Ln, bias=floor_sb[:, g, t:t + 1])
             nc.vector.scalar_tensor_tensor(
-                planes[:, t, :], log_a[:], gain_sb[:, g, t:t + 1], ref_log[g][t][:, first:first + width],
+                planes[:, t, :], log_a[:], gain_sb[:, g, t:t + 1], weighted[g][t][:, first:first + width],
                 ALU.mult, ALU.subtract)
 
         def weave(planes, name):
             width = planes.shape[2]
-            woven = keep.tile([P, width * PACK], BF16, name=name, tag="woven", bufs=2, align_bytes=64)
+            woven = keep.tile([P, width * PACK], BF16, name=name, align_bytes=64)
             nc.vector.tensor_copy(
                 woven[:].rearrange("p (c i t) -> p c t i", i=4, t=PACK),
                 planes.rearrange("p t (c i) -> p c t i", i=4))
@@ -236,19 +243,20 @@ def tile_list_plume_retrieval_kernel(
             finish_a(g, t, jh * HALF, power[:], planes)
             if t == PACK - 1:
                 h_q[g, jh] = weave(planes[:], "h%d%d" % (g, jh))
-                if (g, jh) == (1, 0):
+                if g == 1:
                     for c in range(4):
                         for g_pass in range(2):
                             signals(c, g_pass, h_q[g_pass, 0], slice(0, HALF), banks[4 + c])
-            if (g, jh) == (0, 1):
+            if jh == 1:
                 report(t, banks[4 + t], 0, HALF, False)
 
         order = [("b", 0, 0), ("b", 0, 1), ("b", 1, 0), ("a", 0, 0), ("a", 1, 0), ("a", 0, 1), ("b", 1, 1)]
         waiting = None
         for side, g, jh in order:
             planes = ring.tile([P, PACK, HALF], BF16, name="planes", bufs=2) if side == "a" else None
+            product = product_a if side == "a" else product_b
             for t in range(PACK):
-                power = square((product_a if side == "a" else product_b)(g, t, jh)[:])
+                power = square(product(g, t, jh)[:])
                 if waiting is not None:
                     finish(*waiting)
                 waiting = (side, g, t, jh, power, planes)
@@ -261,13 +269,14 @@ def tile_list_plume_retrieval_kernel(
                 powers.append(square(last[t][:, cols]))
                 if (q, t) == (0, 0):
                     finish(*waiting)
+            first = HALF + q * QUARTER
             for t in range(PACK):
-                finish_a(1, t, HALF + q * QUARTER, powers[t][:], planes)
+                finish_a(1, t, first, powers[t][:], planes)
             h1q = weave(planes[:], "h1q%d" % q)
             for c in range(4):
                 signals(c, 0, h_q[0, 1], cols, banks[4 * (1 - q) + c])
             for c in range(4):
                 signals(c, 1, h1q, slice(0, QUARTER), banks[4 * (1 - q) + c])
-        for q in range(2):
+        for q, on_scalar in ((0, (0, 1)), (1, (1,))):
             for c in range(4):
-                report(c, banks[4 * (1 - q) + c], HALF + q * QUARTER, QUARTER, q == 0)
+                report(c, banks[4 * (1 - q) + c], HALF + q * QUARTER, QUARTER, c in on_scalar)

@@ -135,7 +135,7 @@ def tile_list_plume_retrieval_kernel(
                 (nc.sync if r < 3 else nc.gpsimd).dma_start(
                     out=planes_s[r:P:32, a, :].bitcast(I32),
                     in_=rows_s[LIVE + 16 * a + r:LIVE + 16 * (a + 1):4, :].bitcast(I32))
-        wr_grouped = held([P, PASS * PACK], BF16, "wr_grouped")
+        wr_grouped = held([P, PASS * PACK], BF16, "wr_grouped", tag="tab2_w")
         for u in range(2):
             nc.vector.tensor_copy(*wr_views(wr_raw1, wr_grouped[:, 2 * PASS * u:2 * PASS * (u + 1)], u))
         wr_q.append([quantise(wr_grouped[:], "wr1")])

from contextlib import ExitStack

import concourse.mybir as mybir

T, S, K, K2, H, N = 4096, 1024, 1024, 512, 1024, 512
FLOPS = 2 * S * (K * H + K2 * H + H * N)

F32 = mybir.dt.float32
BF16 = mybir.dt.bfloat16
I32 = mybir.dt.int32
U32 = mybir.dt.uint32
U16 = mybir.dt.uint16
U8 = mybir.dt.uint8
FP8X4 = mybir.dt.float8_e4m3fn_x4
FP4X4 = mybir.dt.float4_e2m1fn_x4
ALU = mybir.AluOpType
ACT = mybir.ActivationFunctionType

P = 128
PACK = 4
PASS = P * PACK
HALF = 512
QUARTER = 256
ROW = S + H + N
LIVE = 96


def tile_list_plume_retrieval_kernel(
    tc, tab_words, tab_scales, tab2_words, tab2_scales, offs, offs2,
    w4_words, w4_scales, wr, x8_words, x8_scales, floor, gain, det, out,
):
    nc = tc.nc
    with ExitStack() as ctx:
        keep = ctx.enter_context(tc.tile_pool(name="keep", bufs=1))
        ring = ctx.enter_context(tc.tile_pool(name="ring", bufs=4))
        stage = ctx.enter_context(tc.tile_pool(name="stage", bufs=1))
        early = ctx.enter_context(tc.tile_pool(name="early", bufs=1))
        psum = ctx.enter_context(tc.psum_pool(name="psum", bufs=1))

        def held(shape, dtype, name, tag=None):
            return keep.tile(shape, dtype, name=name, tag=tag or name, align_bytes=64)

        banks = [psum.tile([P, HALF], F32, name="bank%d" % i) for i in range(8)]

        list2 = keep.tile([P, S // 16], U16, name="list2")
        list1 = keep.tile([P, S // 16], U16, name="list1")
        tab2_s = early.tile([P, T], U8, name="tab2_s", offset=4096, align_bytes=64)
        tab_s = held([P, T], U8, "tab_s")
        weight_s = held([P, H + N], U8, "weight_s")
        planes_s = held([P, 2, ROW], U8, "planes_s")
        by_row = held([P, 2, 2, PACK], F32, "by_row")
        floor_sb, gain_sb = by_row[:, 0], by_row[:, 1]
        neg_det = held([P, 4], F32, "neg_det")

        warm = held([P, 4 * PACK], F32, "warm")
        flat = by_row[:].rearrange("p u g t -> p (u g t)")
        nc.vector.memset(flat, 1.0)
        nc.vector.memset(tab2_s[:].bitcast(I32), 0)
        nc.vector.memset(tab_s[0:LIVE, :].bitcast(I32), 0)
        nc.vector.memset(weight_s[0:LIVE, :].bitcast(I32), 0)

        def load_wr(g, raw):
            nc.sync.dma_start(out=raw[:], in_=wr[:, g * PASS:(g + 1) * PASS].rearrange("(p j) c -> p j c", j=PACK))
            return raw

        def load_tab(a, window):
            nc.sync.dma_start(
                out=window[:].bitcast(I32), in_=tab_words[a].rearrange("p t i -> p (t i)").bitcast(I32))
            return window

        nc.sync.dma_start(list1[:], offs)
        nc.sync.dma_start(list2[:], offs2)
        for rows, scales in ((tab_s[LIVE:P, :], tab_scales), (weight_s[LIVE:P, 0:H], w4_scales),
                             (weight_s[LIVE:P, H:H + N], x8_scales)):
            nc.scalar.dma_start(out=rows.bitcast(I32), in_=scales.rearrange("a q c -> (a q) c").bitcast(I32))
        wr_raw0 = load_wr(0, stage.tile([P, PACK, PASS], F32, name="wr_raw0", offset=14336, align_bytes=64))
        tab2_w = held([P, T], U16, "tab2_w")
        nc.sync.dma_start(out=tab2_w[:].bitcast(I32), in_=tab2_words[0].bitcast(I32))
        nc.scalar.activation(warm[:], flat, ACT.Ln)
        for r in range(4):
            nc.scalar.dma_start(out=tab2_s[r:P:32, :].bitcast(I32), in_=tab2_scales[0, r:16:4, :].bitcast(I32))
        nc.scalar.dma_start(out=floor_sb, in_=floor.rearrange("(g p t) -> p g t", g=2, t=PACK))
        nc.scalar.dma_start(out=gain_sb, in_=gain.rearrange("(g p t) -> p g t", g=2, t=PACK))

        def gather(window, offsets, dtype, name, place=None):
            shape = [P, 16 * offsets.shape[1]]
            if place is None:
                picked = held(shape, dtype, name)
            else:
                picked = early.tile(shape, dtype, name=name, offset=place, align_bytes=64)
            nc.vector.tensor_copy(picked[:], window.indirect(offsets))
            return picked

        def half_of(offsets, jh):
            return offsets[:, jh * (HALF // 16):(jh + 1) * (HALF // 16)]

        def wr_views(raw, pair, u):
            dst = pair.rearrange("p (t m j) -> p m j t", t=2, j=PACK)
            src = raw[:].rearrange("p j (m t) -> p m j t", t=PACK)[:, :, :, 2 * u:2 * u + 2]
            return dst, src

        def quantise(values, name):
            width = values.shape[1] // PACK
            codes = held([P, width], U32, name + "_codes")
            scales = held([P, width], U8, name + "_scales")
            nc.vector.quantize_mx(out=codes[:].bitcast(FP8X4), scales=scales[:], in_=values)
            return codes, scales

        v2_s = [None, None]
        v2_w = [None, None]
        picked_s = gather(tab_s[:], list1[:], U8, "picked_s")
        wr_raw1 = load_wr(1, held([P, PACK, PASS], F32, "wr_raw1", tag="tab_s"))
        v2_s[0] = gather(tab2_s[:], half_of(list2, 0), U8, "v2_s0")
        pairs = [early.tile([P, 2 * PASS], BF16, name="wr_pair%d" % u, offset=2048 * u, align_bytes=64) for u in range(2)]
        for u in range(2):
            nc.scalar.activation(*wr_views(wr_raw0, pairs[u][:], u), ACT.Copy)
        wr_q = [[quantise(pairs[0][:], "wr00")]]
        tab_w = [load_tab(0, stage.tile([P, T], U32, name="tab_w0", offset=0, align_bytes=64))]
        w4_raw = stage.tile([P, 2, H], U16, name="w4_raw", offset=16384, align_bytes=64)
        nc.sync.dma_start(out=w4_raw[:].bitcast(I32), in_=w4_words.rearrange("a p c -> p a c").bitcast(I32))
        tab_w.append(load_tab(1, stage.tile([P, T], U32, name="tab_w1", offset=20480, align_bytes=64)))
        v2_w[0] = gather(tab2_w[:], half_of(list2, 0), U16, "v2_w0")
        wr_q[0].append(quantise(pairs[1][:], "wr01"))
        v2_s[1] = gather(tab2_s[:], half_of(list2, 1), U8, "v2_s1", 2048)
        v2_w[1] = gather(tab2_w[:], half_of(list2, 1), U16, "v2_w1", 4096)
        rows_s = early.tile([P, ROW], U8, name="rows_s", offset=5120, align_bytes=64)
        nc.vector.memset(planes_s[:].rearrange("p a c -> p (a c)").bitcast(I32), 0)
        nc.vector.tensor_copy(
            rows_s[:, S:S + H].rearrange("p (g t o i) -> p g o t i", g=2, t=PACK, i=16),
            weight_s[:, 0:H].rearrange("p (g o i t) -> p g o t i", g=2, t=PACK, i=16))
        nc.vector.tensor_copy(rows_s[:, 0:S].bitcast(I32), picked_s[:].bitcast(I32))
        nc.vector.tensor_copy(rows_s[:, S + H:ROW].bitcast(I32), weight_s[:, H:H + N].bitcast(I32))
        for a in range(2):
            for r in range(4):
                (nc.sync if r < 3 else nc.gpsimd).dma_start(
                    out=planes_s[r:P:32, a, :].bitcast(I32),
                    in_=rows_s[LIVE + 16 * a + r:LIVE + 16 * (a + 1):4, :].bitcast(I32))
        wr_grouped = held([P, PASS * PACK], BF16, "wr_grouped", tag="tab2_w")
        for u in range(2):
            nc.vector.tensor_copy(*wr_views(wr_raw1, wr_grouped[:, 2 * PASS * u:2 * PASS * (u + 1)], u))
        wr_q.append([quantise(wr_grouped[:], "wr1")])

        v_w = [[gather(tab_w[a][:], half_of(list1, 0), U32, "v_w0%d" % a) for a in range(2)]]
        w4_w = held([P, 2 * H], U16, "w4_w")
        nc.vector.tensor_copy(
            w4_w[:].rearrange("p (u t o i) -> p u o t i", u=4, t=PACK, i=8),
            w4_raw[:].rearrange("p a (g o i t) -> p (a g) o t i", g=2, t=PACK, i=8))
        v_w.append([gather(tab_w[a][:], half_of(list1, 1), U32, "v_w1%d" % a) for a in range(2)])
        x8_w = stage.tile([P, 2, N], U32, name="x8_w", offset=16384, align_bytes=64)
        nc.sync.dma_start(out=x8_w[:].bitcast(I32), in_=x8_words.rearrange("a p c i -> p a (c i)").bitcast(I32))
        det_sb = early.tile([P, 4], F32, name="det_sb", offset=5120, align_bytes=64)
        with nc.allow_non_contiguous_dma(reason="one detection limit a partition"):
            nc.sync.dma_start(out=det_sb[:], in_=det.rearrange("(c p) -> p c", p=P))
        nc.gpsimd.tensor_scalar(neg_det[:], det_sb[:], -1.0, 0.0, ALU.mult, ALU.add)

        turn = [0]

        def next_bank():
            turn[0] = (turn[0] + 1) % 4
            return banks[turn[0]]

        def product_b(g, t, jh):
            bank = next_bank()
            per_tile = PACK // len(wr_q[g])
            codes, scales = wr_q[g][t // per_tile]
            cols = slice(t % per_tile * P, (t % per_tile + 1) * P)
            nc.tensor.matmul_mx(
                out=bank[:], lhsT=codes[:, cols].bitcast(FP8X4), lhsT_scale=scales[:, cols],
                rhs=v2_w[jh][:].bitcast(FP4X4), rhs_scale=v2_s[jh][:], start=True, stop=True)
            return bank

        def product_a(g, t, jh):
            bank = next_bank()
            for a in range(2):
                first = g * PASS + t * P
                nc.tensor.matmul_mx(
                    out=bank[:], lhsT=w4_w[:, a * H + first:a * H + first + P].bitcast(FP4X4),
                    lhsT_scale=planes_s[:, a, S + first:S + first + P],
                    rhs=v_w[jh][a][:].bitcast(FP8X4), rhs_scale=planes_s[:, a, jh * HALF:(jh + 1) * HALF],
                    start=(a == 0), stop=(a == 1))
            return bank

        def square(amplitude):
            power = ring.tile([P, amplitude.shape[1]], F32, name="power", bufs=6)
            nc.scalar.activation(power[:], amplitude, ACT.Square)
            return power

        ref_log = [[held([P, S], F32, "ref_log%d%d" % (g, t)) for t in range(PACK)] for g in range(2)]

        weighted = [
            [stage.tile([P, S], F32, name="weighted%d%d" % (g, t), offset=20480 * g + 4096 * t, align_bytes=64)
             for t in range(PACK)] for g in range(2)]

        def finish_b(g, t, jh, power):
            log_b = ref_log[g][t]
            cols = slice(jh * HALF, (jh + 1) * HALF)
            nc.scalar.activation(log_b[:, cols], power[:], ACT.Ln, bias=floor_sb[:, g, t:t + 1])
            if (g, jh) != (0, 0):
                ready = slice(0, S) if g == 0 else cols
                nc.vector.tensor_scalar(
                    weighted[g][t][:, ready], log_b[:, ready], gain_sb[:, g, t:t + 1], None, ALU.mult)

        def finish_a(g, t, first, power, planes):
            width = power.shape[1]
            log_a = ring.tile([P, width], F32, name="log_a", bufs=8)
            nc.scalar.activation(log_a[:], power, ACT.Ln, bias=floor_sb[:, g, t:t + 1])
            nc.vector.scalar_tensor_tensor(
                planes[:, t, :], log_a[:], gain_sb[:, g, t:t + 1], weighted[g][t][:, first:first + width],
                ALU.mult, ALU.subtract)

        def weave(planes, name):
            width = planes.shape[2]
            woven = keep.tile([P, width * PACK], BF16, name=name, align_bytes=64)
            nc.vector.tensor_copy(
                woven[:].rearrange("p (c i t) -> p c t i", i=4, t=PACK),
                planes.rearrange("p t (c i) -> p c t i", i=4))
            return quantise(woven[:], name)

        def signals(c, g, h_q, h_cols, bank):
            codes, scales = h_q
            cols = slice(c * P, (c + 1) * P)
            width = h_cols.stop - h_cols.start
            nc.tensor.matmul_mx(
                out=bank[:, 0:width], lhsT=x8_w[:, g, cols].bitcast(FP8X4), lhsT_scale=planes_s[:, g, S + H + c * P:S + H + (c + 1) * P],
                rhs=codes[:, h_cols].bitcast(FP8X4), rhs_scale=scales[:, h_cols], start=(g == 0), stop=(g == 1))

        def report(c, bank, first, width, on_scalar):
            result = keep.tile([P, width], F32, name="result", tag="result", bufs=8)
            if on_scalar:
                excess = ring.tile([P, width], F32, name="excess")
                nc.scalar.activation(excess[:], bank[:, 0:width], ACT.Relu, bias=neg_det[:, c:c + 1])
                nc.scalar.activation(result[:], excess[:], ACT.Identity, bias=det_sb[:, c:c + 1])
            else:
                nc.vector.tensor_scalar(result[:], bank[:, 0:width], det_sb[:, c:c + 1], None, ALU.max)
            nc.sync.dma_start(out=out[c * P:(c + 1) * P, first:first + width], in_=result[:])

        h_q = {}

        def finish(side, g, t, jh, power, planes):
            if side == "b":
                finish_b(g, t, jh, power)
                return
            finish_a(g, t, jh * HALF, power[:], planes)
            if t == PACK - 1:
                h_q[g, jh] = weave(planes[:], "h%d%d" % (g, jh))
                if g == 1:
                    for c in range(4):
                        for g_pass in range(2):
                            signals(c, g_pass, h_q[g_pass, 0], slice(0, HALF), banks[4 + c])
            if jh == 1:
                report(t, banks[4 + t], 0, HALF, False)

        order = [("b", 0, 0), ("b", 0, 1), ("b", 1, 0), ("a", 0, 0), ("a", 1, 0), ("a", 0, 1), ("b", 1, 1)]
        waiting = None
        for side, g, jh in order:
            planes = ring.tile([P, PACK, HALF], BF16, name="planes", bufs=2) if side == "a" else None
            product = product_a if side == "a" else product_b
            for t in range(PACK):
                power = square(product(g, t, jh)[:])
                if waiting is not None:
                    finish(*waiting)
                waiting = (side, g, t, jh, power, planes)
        last = [product_a(1, t, 1) for t in range(PACK)]
        for q in range(2):
            planes = held([P, PACK, QUARTER], BF16, "planes_q%d" % q)
            cols = slice(q * QUARTER, (q + 1) * QUARTER)
            powers = []
            for t in range(PACK):
                powers.append(square(last[t][:, cols]))
                if (q, t) == (0, 0):
                    finish(*waiting)
            first = HALF + q * QUARTER
            for t in range(PACK):
                finish_a(1, t, first, powers[t][:], planes)
            h1q = weave(planes[:], "h1q%d" % q)
            for c in range(4):
                signals(c, 0, h_q[0, 1], cols, banks[4 * (1 - q) + c])
            for c in range(4):
                signals(c, 1, h1q, slice(0, QUARTER), banks[4 * (1 - q) + c])
        for q, on_scalar in ((0, (0, 1)), (1, (1,))):
            for c in range(4):
                report(c, banks[4 * (1 - q) + c], HALF + q * QUARTER, QUARTER, c in on_scalar)
